import numpy as np
import ml_dtypes

BF16 = ml_dtypes.bfloat16


def bf(x):
    return np.asarray(x, np.float32).astype(BF16)


def f32(x):
    return np.asarray(x, np.float32)


def f64(x):
    return np.asarray(x).astype(np.float64)


def striped(idx):
    return np.tile(idx.reshape(-1, 16).T, (8, 1))


S, K, M, N, E, Q = 1024, 256, 256, 2048, 4, 512


def gelu_tanh(v):
    return 0.5 * v * (1.0 + np.tanh(np.sqrt(2.0 / np.pi) * (v + 0.044715 * v**3)))


def two_experts():
    first = np.random.permutation(S).reshape(E, S // E)
    return np.concatenate([np.random.permutation(np.concatenate([first[e], first[(e + 1) % E]])) for e in range(E)])


def setup_inputs():
    return {"table": bf(np.random.standard_normal((S, K))), "w": bf(np.random.standard_normal((E, K, M)) / np.sqrt(K)), "b": f32(0.5 * np.random.standard_normal((M, 1))), "offs": striped(two_experts())}


def reference(table, w, b, offs):
    idx = offs[:16].T.reshape(-1)
    x = f64(table)[idx].T
    y = np.concatenate([f64(w)[e].T @ x[:, e * Q : (e + 1) * Q] for e in range(E)], axis=1)
    return gelu_tanh(y + f64(b))

@@ -1,0 +1,64 @@
+import concourse.mybir as mybir
+from concourse.masks import make_identity
+
+P = 128
+S = 1024
+K = 256
+M = 256
+E = 4
+Q = 512
+N = E * Q
+K_BLOCKS = K // P
+M_BLOCKS = M // P
+HALF = S // 2
+
+BF16, F32, U16 = mybir.dt.bfloat16, mybir.dt.float32, mybir.dt.uint16
+gelu_tanh = mybir.ActivationFunctionType.Gelu_apprx_tanh
+
+FLOPS = 2 * N * K * M
+
+
+def tile_gather_matmul_kernel(tc, table, w, b, offs, out):
+    nc = tc.nc
+    with (
+        tc.tile_pool(name="held", bufs=1) as held,
+        tc.tile_pool(name="results", bufs=E * M_BLOCKS) as results,
+        tc.psum_pool(name="banks", bufs=8) as banks,
+    ):
+        tokens = held.tile([P, S // P, K], BF16)
+        nc.sync.dma_start(tokens[:], table.rearrange("(n p) k -> p n k", p=P))
+        offsets = held.tile([P, N // 16], U16)
+        nc.sync.dma_start(offsets[:], offs)
+        weights = held.tile([P, E, K_BLOCKS, M], BF16)
+        nc.sync.dma_start(weights[:], w.rearrange("e (kb p) m -> p e kb m", p=P))
+        bias = held.tile([P, M_BLOCKS], F32)
+        nc.scalar.dma_start(bias[:], b.rearrange("(mb p) o -> p (mb o)", p=P))
+
+        identity = held.tile([P, P], BF16)
+        make_identity(nc, identity[:])
+
+        flipped = [held.tile([P, S], BF16, name=f"flipped{kb}") for kb in range(K_BLOCKS)]
+        for kb in range(K_BLOCKS):
+            for first in range(0, S, HALF):
+                turned = banks.tile([P, HALF], BF16, name="turned", tag="bank")
+                for s in range(0, HALF, P):
+                    block = tokens[:, (first + s) // P, kb * P : (kb + 1) * P]
+                    nc.tensor.transpose(turned[:, s : s + P], block, identity[:])
+                nc.vector.tensor_copy(flipped[kb][:, first : first + HALF], turned[:])
+
+        for e in range(E):
+            piece = offsets[:, e * Q // 16 : (e + 1) * Q // 16]
+            sums = [banks.tile([P, Q], F32, name="sums", tag="bank") for mb in range(M_BLOCKS)]
+            for kb in range(K_BLOCKS):
+                for mb in range(M_BLOCKS):
+                    nc.tensor.matmul(
+                        sums[mb][:],
+                        weights[:, e, kb, mb * P : (mb + 1) * P],
+                        flipped[kb][:].indirect(piece),
+                        start=kb == 0,
+                        stop=kb == K_BLOCKS - 1,
+                    )
+            for mb in range(M_BLOCKS):
+                result = results.tile([P, Q], F32)
+                nc.scalar.activation(result[:], sums[mb][:], gelu_tanh, bias=bias[:, mb : mb + 1])
+                nc.sync.dma_start(out[mb * P : (mb + 1) * P, e * Q : (e + 1) * Q], result[:])

@@ -22,11 +22,13 @@ def tile_gather_matmul_kernel(tc, table, w, b, offs, out):
     nc = tc.nc
     with (
         tc.tile_pool(name="held", bufs=1) as held,
-        tc.tile_pool(name="results", bufs=E * M_BLOCKS) as results,
+        tc.tile_pool(name="results", bufs=E * M_BLOCKS + 1) as results,
         tc.psum_pool(name="banks", bufs=8) as banks,
     ):
-        tokens = held.tile([P, S // P, K], BF16)
-        nc.sync.dma_start(tokens[:], table.rearrange("(n p) k -> p n k", p=P))
+        tokens = [held.tile([P, HALF // P, K], BF16, name=f"tokens{h}") for h in range(2)]
+        for h in range(2):
+            half_of_table = table[h * HALF : (h + 1) * HALF, :]
+            nc.sync.dma_start(tokens[h][:], half_of_table.rearrange("(n p) k -> p n k", p=P))
         offsets = held.tile([P, N // 16], U16)
         nc.sync.dma_start(offsets[:], offs)
         weights = held.tile([P, E, K_BLOCKS, M], BF16)
@@ -34,17 +36,23 @@ def tile_gather_matmul_kernel(tc, table, w, b, offs, out):
         bias = held.tile([P, M_BLOCKS], F32)
         nc.scalar.dma_start(bias[:], b.rearrange("(mb p) o -> p (mb o)", p=P))
 
+        zero = held.tile([P, 1], F32)
+        nc.vector.memset(zero[:], 0.0)
+        gelu_of_zero = held.tile([P, 1], F32)
+        nc.scalar.activation(gelu_of_zero[:], zero[:], gelu_tanh)
+
         identity = held.tile([P, P], BF16)
         make_identity(nc, identity[:])
 
         flipped = [held.tile([P, S], BF16, name=f"flipped{kb}") for kb in range(K_BLOCKS)]
-        for kb in range(K_BLOCKS):
-            for first in range(0, S, HALF):
+        copy_out = [nc.vector.tensor_copy, nc.scalar.copy]
+        for h in range(2):
+            for kb in range(K_BLOCKS):
                 turned = banks.tile([P, HALF], BF16, name="turned", tag="bank")
-                for s in range(0, HALF, P):
-                    block = tokens[:, (first + s) // P, kb * P : (kb + 1) * P]
-                    nc.tensor.transpose(turned[:, s : s + P], block, identity[:])
-                nc.vector.tensor_copy(flipped[kb][:, first : first + HALF], turned[:])
+                for n in range(HALF // P):
+                    block = tokens[h][:, n, kb * P : (kb + 1) * P]
+                    nc.tensor.transpose(turned[:, n * P : (n + 1) * P], block, identity[:])
+                copy_out[kb](flipped[kb][:, h * HALF : (h + 1) * HALF], turned[:])
 
         for e in range(E):
             piece = offsets[:, e * Q // 16 : (e + 1) * Q // 16]
@@ -59,6 +67,9 @@ def tile_gather_matmul_kernel(tc, table, w, b, offs, out):
                         stop=kb == K_BLOCKS - 1,
                     )
             for mb in range(M_BLOCKS):
-                result = results.tile([P, Q], F32)
-                nc.scalar.activation(result[:], sums[mb][:], gelu_tanh, bias=bias[:, mb : mb + 1])
-                nc.sync.dma_start(out[mb * P : (mb + 1) * P, e * Q : (e + 1) * Q], result[:])
+                parts = 2 if (e, mb) == (E - 1, M_BLOCKS - 1) else 1
+                width = Q // parts
+                for j in range(0, Q, width):
+                    result = results.tile([P, width], F32, name="result")
+                    nc.scalar.activation(result[:], sums[mb][:, j : j + width], gelu_tanh, bias=bias[:, mb : mb + 1])
+                    nc.sync.dma_start(out[mb * P : (mb + 1) * P, e * Q + j : e * Q + j + width], result[:])

@@ -31,10 +31,12 @@ def tile_gather_matmul_kernel(tc, table, w, b, offs, out):
             nc.sync.dma_start(tokens[h][:], half_of_table.rearrange("(n p) k -> p n k", p=P))
         offsets = held.tile([P, N // 16], U16)
         nc.sync.dma_start(offsets[:], offs)
-        weights = held.tile([P, E, K_BLOCKS, M], BF16)
-        nc.sync.dma_start(weights[:], w.rearrange("e (kb p) m -> p e kb m", p=P))
+        weights = [held.tile([P, K_BLOCKS, M], BF16, name=f"weights{e}") for e in range(E)]
         bias = held.tile([P, M_BLOCKS], F32)
-        nc.scalar.dma_start(bias[:], b.rearrange("(mb p) o -> p (mb o)", p=P))
+        for e in range(E):
+            nc.sync.dma_start(weights[e][:], w[e, :, :].rearrange("(kb p) m -> p kb m", p=P))
+            if e == 0:
+                nc.sync.dma_start(bias[:], b.rearrange("(mb p) o -> p (mb o)", p=P))
 
         zero = held.tile([P, 1], F32)
         nc.vector.memset(zero[:], 0.0)
@@ -56,20 +58,19 @@ def tile_gather_matmul_kernel(tc, table, w, b, offs, out):
 
         for e in range(E):
             piece = offsets[:, e * Q // 16 : (e + 1) * Q // 16]
-            sums = [banks.tile([P, Q], F32, name="sums", tag="bank") for mb in range(M_BLOCKS)]
-            for kb in range(K_BLOCKS):
-                for mb in range(M_BLOCKS):
+            for mb in range(M_BLOCKS):
+                sums = banks.tile([P, Q], F32, name="sums", tag="bank")
+                for kb in range(K_BLOCKS):
                     nc.tensor.matmul(
-                        sums[mb][:],
-                        weights[:, e, kb, mb * P : (mb + 1) * P],
+                        sums[:],
+                        weights[e][:, kb, mb * P : (mb + 1) * P],
                         flipped[kb][:].indirect(piece),
                         start=kb == 0,
                         stop=kb == K_BLOCKS - 1,
                     )
-            for mb in range(M_BLOCKS):
                 parts = 2 if (e, mb) == (E - 1, M_BLOCKS - 1) else 1
                 width = Q // parts
                 for j in range(0, Q, width):
                     result = results.tile([P, width], F32, name="result")
-                    nc.scalar.activation(result[:], sums[mb][:, j : j + width], gelu_tanh, bias=bias[:, mb : mb + 1])
+                    nc.scalar.activation(result[:], sums[:, j : j + width], gelu_tanh, bias=bias[:, mb : mb + 1])
                     nc.sync.dma_start(out[mb * P : (mb + 1) * P, e * Q + j : e * Q + j + width], result[:])

@@ -11,6 +11,7 @@ N = E * Q
 K_BLOCKS = K // P
 M_BLOCKS = M // P
 HALF = S // 2
+WARM_UP_MATMULS = 16
 
 BF16, F32, U16 = mybir.dt.bfloat16, mybir.dt.float32, mybir.dt.uint16
 gelu_tanh = mybir.ActivationFunctionType.Gelu_apprx_tanh
@@ -38,10 +39,13 @@ def tile_gather_matmul_kernel(tc, table, w, b, offs, out):
             if e == 0:
                 nc.sync.dma_start(bias[:], b.rearrange("(mb p) o -> p (mb o)", p=P))
 
-        zero = held.tile([P, 1], F32)
-        nc.vector.memset(zero[:], 0.0)
+        zeros = held.tile([P, P], BF16)
+        nc.gpsimd.memset(zeros[:], 0.0)
+        unread = banks.tile([P, P], F32, name="unread", tag="bank")
+        for i in range(WARM_UP_MATMULS):
+            nc.tensor.matmul(unread[:], zeros[:], zeros[:], start=True, stop=True)
         gelu_of_zero = held.tile([P, 1], F32)
-        nc.scalar.activation(gelu_of_zero[:], zero[:], gelu_tanh)
+        nc.scalar.activation(gelu_of_zero[:], zeros[:, :1], gelu_tanh)
 
         identity = held.tile([P, P], BF16)
         make_identity(nc, identity[:])

import concourse.mybir as mybir
from concourse.masks import make_identity

P = 128
S = 1024
K = 256
M = 256
E = 4
Q = 512
N = E * Q
K_BLOCKS = K // P
M_BLOCKS = M // P
HALF = S // 2
WARM_UP_MATMULS = 16

BF16, F32, U16 = mybir.dt.bfloat16, mybir.dt.float32, mybir.dt.uint16
gelu_tanh = mybir.ActivationFunctionType.Gelu_apprx_tanh

FLOPS = 2 * N * K * M


def tile_gather_matmul_kernel(tc, table, w, b, offs, out):
    nc = tc.nc
    with (
        tc.tile_pool(name="held", bufs=1) as held,
        tc.tile_pool(name="results", bufs=E * M_BLOCKS + 1) as results,
        tc.psum_pool(name="banks", bufs=8) as banks,
    ):
        tokens = [held.tile([P, HALF // P, K], BF16, name=f"tokens{h}") for h in range(2)]
        for h in range(2):
            half_of_table = table[h * HALF : (h + 1) * HALF, :]
            nc.sync.dma_start(tokens[h][:], half_of_table.rearrange("(n p) k -> p n k", p=P))
        offsets = held.tile([P, N // 16], U16)
        nc.sync.dma_start(offsets[:], offs)
        weights = [held.tile([P, K_BLOCKS, M], BF16, name=f"weights{e}") for e in range(E)]
        bias = held.tile([P, M_BLOCKS], F32)
        for e in range(E):
            nc.sync.dma_start(weights[e][:], w[e, :, :].rearrange("(kb p) m -> p kb m", p=P))
            if e == 0:
                nc.sync.dma_start(bias[:], b.rearrange("(mb p) o -> p (mb o)", p=P))

        zeros = held.tile([P, P], BF16)
        nc.gpsimd.memset(zeros[:], 0.0)
        unread = banks.tile([P, P], F32, name="unread", tag="bank")
        for i in range(WARM_UP_MATMULS):
            nc.tensor.matmul(unread[:], zeros[:], zeros[:], start=True, stop=True)
        gelu_of_zero = held.tile([P, 1], F32)
        nc.scalar.activation(gelu_of_zero[:], zeros[:, :1], gelu_tanh)

        identity = held.tile([P, P], BF16)
        make_identity(nc, identity[:])

        flipped = [held.tile([P, S], BF16, name=f"flipped{kb}") for kb in range(K_BLOCKS)]
        copy_out = [nc.vector.tensor_copy, nc.scalar.copy]
        for h in range(2):
            for kb in range(K_BLOCKS):
                turned = banks.tile([P, HALF], BF16, name="turned", tag="bank")
                for n in range(HALF // P):
                    block = tokens[h][:, n, kb * P : (kb + 1) * P]
                    nc.tensor.transpose(turned[:, n * P : (n + 1) * P], block, identity[:])
                copy_out[kb](flipped[kb][:, h * HALF : (h + 1) * HALF], turned[:])

        for e in range(E):
            piece = offsets[:, e * Q // 16 : (e + 1) * Q // 16]
            for mb in range(M_BLOCKS):
                sums = banks.tile([P, Q], F32, name="sums", tag="bank")
                for kb in range(K_BLOCKS):
                    nc.tensor.matmul(
                        sums[:],
                        weights[e][:, kb, mb * P : (mb + 1) * P],
                        flipped[kb][:].indirect(piece),
                        start=kb == 0,
                        stop=kb == K_BLOCKS - 1,
                    )
                parts = 2 if (e, mb) == (E - 1, M_BLOCKS - 1) else 1
                width = Q // parts
                for j in range(0, Q, width):
                    result = results.tile([P, width], F32, name="result")
                    nc.scalar.activation(result[:], sums[:, j : j + width], gelu_tanh, bias=bias[:, mb : mb + 1])
                    nc.sync.dma_start(out[mb * P : (mb + 1) * P, e * Q + j : e * Q + j + width], result[:])
